import numpy as np
import ml_dtypes


def mxq(x, axis, fmt="e4m3"):
    dtype, down = {"e4m3": (ml_dtypes.float8_e4m3fn, 7), "e5m2": (ml_dtypes.float8_e5m2, 14)}[fmt]
    v = np.moveaxis(np.asarray(x, np.float32).astype(ml_dtypes.bfloat16).astype(np.float64), axis, -1)
    blocks = v.reshape(v.shape[:-1] + (-1, 32))
    amax = np.abs(blocks).max(-1, keepdims=True)
    byte = np.maximum(np.where(amax > 0, np.frexp(amax)[1] - 1 + 127, 0) - down, 1)
    scale = np.exp2(byte - 127.0)
    codes = (blocks / scale).astype(np.float32).astype(dtype).astype(np.float64)
    return np.moveaxis((codes * scale).reshape(v.shape), -1, axis)


WIDE = False


def mx_kscale(k):
    if not WIDE:
        return np.ones(k)
    levels = np.array([10, -10, 5, -5, 0])
    if k % 512:
        return np.exp2(np.random.permutation(np.resize(levels, k // 32))).repeat(32)
    a = np.empty((k // 512, 16))
    for p in range(k // 512):
        a[p, :8] = np.random.permutation(np.resize(levels, 8))
        for g in range(8):
            far = levels[np.abs(levels - a[p, g]) >= 10]
            a[p, g + 8] = far[np.random.randint(len(far))]
    return np.exp2(a.ravel()).repeat(32)


BF16 = ml_dtypes.bfloat16


def bf(x):
    return np.asarray(x, np.float32).astype(BF16)


def f64(x):
    return np.asarray(x).astype(np.float64)


E2M1 = np.array([0.0, 0.5, 1.0, 1.5, 2.0, 3.0, 4.0, 6.0, -0.0, -0.5, -1.0, -1.5, -2.0, -3.0, -4.0, -6.0])


def pack_weight(w, fmt):
    k, n = w.shape
    w = f64(bf(w)).reshape(k // 32, 32, n)
    amax = np.abs(w).max(1)
    if fmt == "e4m3":
        byte = np.frexp(amax)[1] - 1 + 127 - 7
    else:
        mant, ex = np.frexp(amax / 6.0)
        byte = np.where(mant > 0.5, ex, ex - 1) + 127
    byte = np.clip(np.where(amax > 0, byte, 1), 1, 254)
    scaled = (w * np.exp2(127.0 - byte)[:, None, :]).reshape(k, n).astype(np.float32)
    by_word = np.ascontiguousarray(scaled.reshape(k // 512, 128, 4, n).transpose(0, 1, 3, 2))
    if fmt == "e4m3":
        words = by_word.astype(ml_dtypes.float8_e4m3fn).view(np.uint8)
    else:
        c = by_word.astype(ml_dtypes.float4_e2m1fn).view(np.uint8) & 0xF
        words = c[..., 0::2] | (c[..., 1::2] << 4)
    return np.ascontiguousarray(words), np.ascontiguousarray(byte.astype(np.uint8).reshape(k // 512, 16, n))


def unpack_weight(words, scales, fmt):
    g, p, n, _ = words.shape
    if fmt == "e4m3":
        vals = np.ascontiguousarray(words).view(ml_dtypes.float8_e4m3fn).astype(np.float64)
    else:
        nib = np.empty((g, p, n, 4), np.uint8)
        nib[..., 0::2] = words & 0xF
        nib[..., 1::2] = words >> 4
        vals = E2M1[nib]
    vals = vals * np.repeat(np.exp2(scales.astype(np.float64) - 127.0), 8, axis=1)[..., None]
    return vals.transpose(0, 1, 3, 2).reshape(g * 512, n)
def pack4(w):
    words, scales = pack_weight(w, "e2m1")
    return words.reshape(words.shape[0], 128, -1), scales


def unpack4(words, scales):
    return unpack_weight(words.reshape(words.shape[0], 128, -1, 2), scales, "e2m1")


def planes(Y):
    n, m = Y.shape
    b = f64(bf(Y)).reshape(n // 32, 32, m)
    amax = np.abs(b).max(1)
    byte = np.clip(np.where(amax > 0, np.frexp(amax)[1] - 1 + 127 - 7, 1), 1, 254)
    codes = (b * np.exp2(127.0 - byte)[:, None, :]).reshape(n, m).astype(np.float32).astype(ml_dtypes.float8_e4m3fn).view(np.uint8)
    words = codes.reshape(n // 512, 128, 4, m).transpose(0, 1, 3, 2)
    return np.ascontiguousarray(words), np.ascontiguousarray(byte.astype(np.uint8).reshape(n // 512, 16, m))


T, K, N = 1024, 1024, 1536

SPREAD = 0.4
STRAY = 0.6


def fresnel_phase(u, v):
    return np.pi * K * (u - v) ** 2


def setup_inputs():
    s = mx_kscale(K)[:, None]
    u = np.random.rand(K, 1)
    v = np.random.rand(1, N)
    a = np.exp(SPREAD * np.random.randn(1, N))
    phase = fresnel_phase(u, v)
    x = np.random.randn(K, T)
    c = a * np.cos(phase) / np.sqrt(K)
    sn = a * np.sin(phase) / np.sqrt(K)
    w = STRAY * a * a * np.random.randn(K, N) / np.sqrt(K)
    x_words, x_scales = pack_weight(f64(bf(x * s)), "e4m3")
    c_words, c_scales = pack_weight(f64(bf(c / s)), "e4m3")
    w_words, w_scales = pack4(f64(bf(w / s)))
    return {"x_words": x_words, "x_scales": x_scales,
            "c_words": c_words, "c_scales": c_scales,
            "w_words": w_words, "w_scales": w_scales,
            "sin_mat": bf(sn / s)}


def reference(x_words, x_scales, c_words, c_scales, w_words, w_scales, sin_mat):
    X = unpack_weight(x_words, x_scales, "e4m3")
    C = unpack_weight(c_words, c_scales, "e4m3")
    W = unpack4(w_words, w_scales)
    S = mxq(f64(sin_mat), 0, "e4m3")
    re = X.T @ C
    im = X.T @ S
    lin = X.T @ W
    y = re * re + im * im + lin
    words, scales = planes(y.T)
    return y, words, scales

@@ -1,0 +1,299 @@
+from contextlib import ExitStack
+
+import concourse.mybir as mybir
+from concourse.masks import make_identity
+
+T, K, N = 1024, 1024, 1536
+FLOPS = 3 * 2 * T * K * N
+
+F32 = mybir.dt.float32
+BF16 = mybir.dt.bfloat16
+I32 = mybir.dt.int32
+U32 = mybir.dt.uint32
+U8 = mybir.dt.uint8
+FP8X4 = mybir.dt.float8_e4m3fn_x4
+FP4X4 = mybir.dt.float4_e2m1fn_x4
+ADD = mybir.AluOpType.add
+SQUARE = mybir.ActivationFunctionType.Square
+
+P = 128
+PACK = 4
+PASSES = K // (P * PACK)
+CHUNK = 512
+CHUNKS = N // CHUNK
+TILES = T // P
+UNITS = CHUNKS * TILES
+QUADS = 4
+X_LOADS = ((0, 256), (256, 512), (512, 1024))
+HEAD_VECTOR_COLS = 320
+VECTOR_COLS = 192
+RUN = 4
+RUN_LAG = 3
+
+
+def tile_fresnel_intensity_plus_linear_k3_kernel(
+    tc, x_words, x_scales, c_words, c_scales, w_words, w_scales, sin_mat, out_0, out_1, out_2
+):
+    nc = tc.nc
+    with ExitStack() as ctx:
+        keep = ctx.enter_context(tc.tile_pool(name="keep", bufs=1))
+        psum = ctx.enter_context(tc.psum_pool(name="psum", bufs=1))
+        ctx.enter_context(tc.manual_schedule())
+
+        def tiles(pool, name, count, shape, dtype):
+            return [pool.tile(shape, dtype, name="%s%d" % (name, i)) for i in range(count)]
+
+        def sbuf(name, count, shape, dtype):
+            return [keep.tile(shape, dtype, name="%s%d" % (name, i), align_bytes=64) for i in range(count)]
+
+        x_codes = [keep.tile([P, PASSES, b - a], U32, name="x%d" % a, align_bytes=64) for a, b in X_LOADS]
+        c_codes = sbuf("c", CHUNKS, [P, PASSES, CHUNK], U32)
+        w_codes = sbuf("w", CHUNKS, [P, PASSES, 2 * CHUNK], U8)
+        xc_plane = keep.tile([P, PASSES * T], U8, align_bytes=64)
+        w_plane = keep.tile([P, PASSES * N], U8, align_bytes=64)
+        s_rows = sbuf("s_rows", CHUNKS * PASSES, [P, PACK, CHUNK], BF16)
+        s_side = sbuf("s_side", CHUNKS * PASSES, [P, CHUNK * PACK], BF16)
+        s_codes = sbuf("s_codes", CHUNKS * PASSES, [P, CHUNK], U32)
+        s_plane = sbuf("s_plane", CHUNKS * PASSES, [P, CHUNK], U8)
+        re_sq = sbuf("re_sq", 3, [P, CHUNK], F32)
+        im_sq = sbuf("im_sq", 3, [P, CHUNK], F32)
+        y_f32 = sbuf("y_f32", 8, [P, CHUNK], F32)
+        y_bf = sbuf("y_bf", 8, [P, CHUNK], BF16)
+        y_side = sbuf("y_side", 3, [P, RUN * P * PACK], BF16)
+        y_codes = sbuf("y_codes", CHUNKS, [P, T], U32)
+        y_plane = sbuf("y_plane", CHUNKS, [P, T], U8)
+        ident = keep.tile([P, P], F32, align_bytes=64)
+        sq_banks = tiles(psum, "sq_bank", 4, [P, CHUNK], F32)
+        lin_banks = tiles(psum, "lin_bank", 2, [P, CHUNK], F32)
+        turn_banks = tiles(psum, "turn_bank", 2, [P, CHUNK], F32)
+
+        x_src = x_words.rearrange("g p m t -> p g (m t)")
+        c_src = c_words.rearrange("g p n t -> p g (n t)")
+        w_src = w_words.rearrange("g p b -> p g b")
+
+        def load_x(i):
+            a, b = X_LOADS[i]
+            nc.sync.dma_start(out=x_codes[i][:].bitcast(I32), in_=x_src[:, :, PACK * a : PACK * b].bitcast(I32))
+
+        def load_c(c):
+            cols = slice(PACK * CHUNK * c, PACK * CHUNK * (c + 1))
+            nc.sync.dma_start(out=c_codes[c][:].bitcast(I32), in_=c_src[:, :, cols].bitcast(I32))
+
+        def load_w(c):
+            cols = slice(2 * CHUNK * c, 2 * CHUNK * (c + 1))
+            nc.sync.dma_start(out=w_codes[c][:].bitcast(I32), in_=w_src[:, :, cols].bitcast(I32))
+
+        def load_s(c):
+            for g in range(PASSES):
+                rows = sin_mat[g * P * PACK : (g + 1) * P * PACK, c * CHUNK : (c + 1) * CHUNK]
+                nc.sync.dma_start(out=s_rows[PASSES * c + g][:], in_=rows.rearrange("(p t) n -> p t n", t=PACK))
+
+        def load_plane_side_by_side(plane, scales):
+            for q in range(QUADS):
+                nc.sync.dma_start(
+                    out=plane[32 * q : 32 * q + 4, :].bitcast(I32).rearrange("r (g n) -> r g n", g=PASSES),
+                    in_=scales[:, 4 * q : 4 * q + 4, :].bitcast(I32).rearrange("g r n -> r g n"),
+                )
+
+        nc.vector.memset(xc_plane[:].bitcast(U32), 0)
+        nc.vector.memset(w_plane[:].bitcast(U32), 0)
+        nc.vector.memset(ident[:], 0.0)
+        make_identity(nc, ident[:], nomemset=True)
+
+        load_plane_side_by_side(xc_plane, x_scales)
+        load_x(0)
+        load_c(0)
+        for q in range(QUADS):
+            nc.sync.dma_start(
+                out=xc_plane[32 * q + 4 : 32 * q + 12, :N].bitcast(I32),
+                in_=c_scales[:, 4 * q : 4 * q + 4, :].bitcast(I32),
+            )
+        load_s(0)
+        load_plane_side_by_side(w_plane, w_scales)
+        load_w(0)
+        load_x(1)
+        load_s(1)
+        load_x(2)
+        load_c(1)
+        load_w(1)
+        load_s(2)
+        load_c(2)
+        load_w(2)
+
+        def product(bank, unit, moving):
+            row = unit % TILES
+            i = max(j for j, (a, b) in enumerate(X_LOADS) if a <= row * P)
+            m0 = row * P - X_LOADS[i][0]
+            for g in range(PASSES):
+                codes, plane = moving(unit // TILES, g)
+                nc.tensor.matmul_mx(
+                    out=bank[:],
+                    lhsT=x_codes[i][:, g, m0 : m0 + P].bitcast(FP8X4),
+                    lhsT_scale=xc_plane[:, g * T + row * P : g * T + (row + 1) * P],
+                    rhs=codes,
+                    rhs_scale=plane,
+                    start=(g == 0),
+                    stop=(g == PASSES - 1),
+                )
+
+        def c_operand(c, g):
+            return c_codes[c][:, g, :].bitcast(FP8X4), xc_plane[4 + 4 * g :, c * CHUNK : (c + 1) * CHUNK]
+
+        def s_operand(c, g):
+            return s_codes[PASSES * c + g][:].bitcast(FP8X4), s_plane[PASSES * c + g][:]
+
+        def w_operand(c, g):
+            return w_codes[c][:, g, :].bitcast(FP4X4), w_plane[:, g * N + c * CHUNK : g * N + (c + 1) * CHUNK]
+
+        def re_bank(u):
+            return sq_banks[(2 * u) % 4]
+
+        def im_bank(u):
+            return sq_banks[(2 * u + 1) % 4]
+
+        def square(dst, bank):
+            nc.scalar.activation(out=dst[:], in_=bank[:], func=SQUARE)
+
+        def interleave(copy, j, a, b):
+            copy(
+                out=s_side[j][:, PACK * a : PACK * b].rearrange("p (c i t) -> p c t i", i=4, t=PACK),
+                in_=s_rows[j][:, :, a:b].rearrange("p t (c i) -> p c t i", i=4),
+            )
+
+        def quantise_s(j):
+            nc.vector.quantize_mx(out=s_codes[j][:].bitcast(FP8X4), scales=s_plane[j][:], in_=s_side[j][:])
+
+        def add(out, in0, in1):
+            nc.vector.tensor_tensor(out=out, in0=in0, in1=in1, op=ADD)
+
+        def store_y(u):
+            c, row = divmod(u, TILES)
+            nc.sync.dma_start(out=out_0[row * P : (row + 1) * P, c * CHUNK : (c + 1) * CHUNK], in_=y_f32[u % 8][:])
+
+        def pair_sorted(ap):
+            return ap.rearrange("m (p u e) -> m u p e", u=2, e=2)
+
+        def round_y(u):
+            nc.vector.tensor_copy(
+                out=y_bf[u % 8][:].rearrange("m (u p e) -> m u p e", u=2, e=2), in_=pair_sorted(y_f32[u % 8][:])
+            )
+
+        def turn(u, bank, place):
+            words = y_bf[u % 8][:].bitcast(F32)
+            for half in range(2):
+                cols = slice((2 * place + half) * P, (2 * place + half + 1) * P)
+                nc.tensor.transpose(bank[:, cols], words[:, half * P : (half + 1) * P], ident[:])
+
+        def empty_turned(bank, count, side, place):
+            nc.scalar.copy(
+                out=side[:, place * P * PACK : (place + count) * P * PACK]
+                .bitcast(F32)
+                .rearrange("p (i m u) -> p i m u", u=2, m=P),
+                in_=bank[:, : count * 2 * P].rearrange("p (i u m) -> p i m u", u=2, m=P),
+            )
+
+        def quantise_y(first, count, side):
+            c, row = divmod(first, TILES)
+            toks = slice(row * P, (row + count) * P)
+            nc.vector.quantize_mx(
+                out=y_codes[c][:, toks].bitcast(FP8X4), scales=y_plane[c][:, toks], in_=side[:, : count * P * PACK]
+            )
+
+        def store_codes(first, count):
+            c, row = divmod(first, TILES)
+            dst = out_1[c].rearrange("p m t -> p (m t)")[:, PACK * row * P : PACK * (row + count) * P]
+            nc.sync.dma_start(out=dst.bitcast(I32), in_=y_codes[c][:, row * P : (row + count) * P].bitcast(I32))
+
+        def store_plane(c, engines):
+            for q in range(QUADS):
+                engines[q % len(engines)].dma_start(
+                    out=out_2[c, 4 * q : 4 * q + 4, :].bitcast(I32),
+                    in_=y_plane[c][32 * q : 32 * q + 4, :].bitcast(I32),
+                )
+
+        product(re_bank(0), 0, c_operand)
+        square(re_sq[0], re_bank(0))
+        product(re_bank(1), 1, c_operand)
+        for g in range(PASSES):
+            interleave(nc.vector.tensor_copy, g, 0, HEAD_VECTOR_COLS)
+            interleave(nc.scalar.copy, g, HEAD_VECTOR_COLS, CHUNK)
+        square(re_sq[1], re_bank(1))
+        for g in range(PASSES):
+            quantise_s(g)
+        for u in range(2):
+            product(lin_banks[u], u, w_operand)
+            add(re_sq[u][:], lin_banks[u][:], re_sq[u][:])
+        for u in range(2):
+            product(im_bank(u), u, s_operand)
+            square(im_sq[u], im_bank(u))
+            add(y_f32[u][:], re_sq[u][:], im_sq[u][:])
+            store_y(u)
+        round_y(0)
+
+        run_units = [first + RUN - 1 + RUN_LAG for first in range(0, UNITS - RUN, RUN)]
+        scalar_jobs = {}
+        vector_jobs = {}
+        share = (CHUNK - VECTOR_COLS) // 2
+        for c in range(1, CHUNKS):
+            free = [u for u in range(max(2, (c - 1) * TILES), c * TILES) if u not in run_units]
+            for g in range(PASSES):
+                j = PASSES * c + g
+                scalar_jobs[free[2 * g]] = (j, VECTOR_COLS, VECTOR_COLS + share)
+                scalar_jobs[free[2 * g + 1]] = (j, VECTOR_COLS + share, CHUNK)
+                vector_jobs.setdefault(free[2 * g], []).append(("interleave", j))
+                vector_jobs.setdefault(free[2 * g + 1], []).append(("quantise", j))
+
+        last = UNITS - 1
+        for u in range(2, UNITS):
+            first = u - RUN_LAG - RUN + 1
+            side = y_side[(first // RUN) % 2]
+            if u in run_units:
+                for i in range(RUN):
+                    turn(first + i, turn_banks[i // 2], i % 2)
+                empty_turned(turn_banks[0], 2, side, 0)
+            product(re_bank(u), u, c_operand)
+            square(re_sq[u % 3], re_bank(u))
+            if u in run_units:
+                empty_turned(turn_banks[1], 2, side, 2)
+            product(im_bank(u), u, s_operand)
+            square(im_sq[u % 3], im_bank(u))
+            if u in scalar_jobs:
+                interleave(nc.scalar.copy, *scalar_jobs[u])
+            product(lin_banks[u % 2], u, w_operand)
+            add(re_sq[u % 3][:], re_sq[u % 3][:], im_sq[u % 3][:])
+            round_y(u - 1)
+            if u == last:
+                break
+            add(y_f32[u % 8][:], lin_banks[u % 2][:], re_sq[u % 3][:])
+            store_y(u)
+            if u in run_units:
+                quantise_y(first, RUN, side)
+                store_codes(first, RUN)
+                if (first + RUN) % TILES == 0:
+                    store_plane(first // TILES, [nc.sync])
+            for kind, j in vector_jobs.get(u, []):
+                if kind == "interleave":
+                    interleave(nc.vector.tensor_copy, j, 0, VECTOR_COLS)
+                else:
+                    quantise_s(j)
+
+        side = y_side[((UNITS - RUN) // RUN) % 2]
+        for i in range(2):
+            turn(UNITS - RUN + i, turn_banks[0], i)
+        empty_turned(turn_banks[0], 2, side, 0)
+        add(
+            y_bf[last % 8][:].rearrange("m (u p e) -> m u p e", u=2, e=2),
+            pair_sorted(lin_banks[last % 2][:]),
+            pair_sorted(re_sq[last % 3][:]),
+        )
+        add(y_f32[last % 8][:], lin_banks[last % 2][:], re_sq[last % 3][:])
+        store_y(last)
+        turn(last - 1, turn_banks[1], 0)
+        empty_turned(turn_banks[1], 1, y_side[2], 0)
+        turn(last, sq_banks[0], 0)
+        empty_turned(sq_banks[0], 1, y_side[2], 1)
+        quantise_y(UNITS - RUN, 2, side)
+        store_codes(UNITS - RUN, 2)
+        quantise_y(last - 1, 2, y_side[2])
+        store_codes(last - 1, 2)
+        store_plane(CHUNKS - 1, [nc.scalar, nc.sync])

@@ -21,14 +21,20 @@ PACK = 4
 PASSES = K // (P * PACK)
 CHUNK = 512
 CHUNKS = N // CHUNK
-TILES = T // P
-UNITS = CHUNKS * TILES
-QUADS = 4
-X_LOADS = ((0, 256), (256, 512), (512, 1024))
-HEAD_VECTOR_COLS = 320
+ROW_TILES = T // P
+PAIRS = CHUNKS * ROW_TILES // 2
+X_HALF = T // 2
+QUADRANT = 32
+LIVE = 4
+QUADRANT_ORDER = (0, 2, 1, 3)
+
+VECTOR_COLS_FIRST = 320
 VECTOR_COLS = 192
-RUN = 4
-RUN_LAG = 3
+PAUSE = 8
+
+PART_DEPTH = 3
+IM_DEPTH = 2
+Y_DEPTH = 4
 
 
 def tile_fresnel_intensity_plus_linear_k3_kernel(
@@ -40,260 +46,291 @@ def tile_fresnel_intensity_plus_linear_k3_kernel(
         psum = ctx.enter_context(tc.psum_pool(name="psum", bufs=1))
         ctx.enter_context(tc.manual_schedule())
 
-        def tiles(pool, name, count, shape, dtype):
-            return [pool.tile(shape, dtype, name="%s%d" % (name, i)) for i in range(count)]
-
         def sbuf(name, count, shape, dtype):
             return [keep.tile(shape, dtype, name="%s%d" % (name, i), align_bytes=64) for i in range(count)]
 
-        x_codes = [keep.tile([P, PASSES, b - a], U32, name="x%d" % a, align_bytes=64) for a, b in X_LOADS]
-        c_codes = sbuf("c", CHUNKS, [P, PASSES, CHUNK], U32)
-        w_codes = sbuf("w", CHUNKS, [P, PASSES, 2 * CHUNK], U8)
-        xc_plane = keep.tile([P, PASSES * T], U8, align_bytes=64)
-        w_plane = keep.tile([P, PASSES * N], U8, align_bytes=64)
+        def banks(name, count):
+            return [psum.tile([P, CHUNK], F32, name="%s%d" % (name, i)) for i in range(count)]
+
+        x_codes = sbuf("x_codes", 2, [P, PASSES, X_HALF], U32)
+        c_codes = sbuf("c_codes", CHUNKS, [P, PASSES, CHUNK], U32)
+        w_codes = sbuf("w_codes", CHUNKS, [P, PASSES, 2 * CHUNK], U8)
+        x_plane = keep.tile([P, PASSES * T], U8, align_bytes=64)
+        c_plane = keep.tile([P, N], U8, align_bytes=64)
+        w_plane_first = keep.tile([P, PASSES * CHUNK], U8, align_bytes=64)
+        w_plane_rest = keep.tile([P, PASSES * (N - CHUNK)], U8, align_bytes=64)
         s_rows = sbuf("s_rows", CHUNKS * PASSES, [P, PACK, CHUNK], BF16)
         s_side = sbuf("s_side", CHUNKS * PASSES, [P, CHUNK * PACK], BF16)
         s_codes = sbuf("s_codes", CHUNKS * PASSES, [P, CHUNK], U32)
         s_plane = sbuf("s_plane", CHUNKS * PASSES, [P, CHUNK], U8)
-        re_sq = sbuf("re_sq", 3, [P, CHUNK], F32)
-        im_sq = sbuf("im_sq", 3, [P, CHUNK], F32)
-        y_f32 = sbuf("y_f32", 8, [P, CHUNK], F32)
-        y_bf = sbuf("y_bf", 8, [P, CHUNK], BF16)
-        y_side = sbuf("y_side", 3, [P, RUN * P * PACK], BF16)
+        part = sbuf("part", PART_DEPTH, [P, 2, CHUNK], F32)
+        im_sq = sbuf("im_sq", IM_DEPTH, [P, 2, CHUNK], F32)
+        y_f32 = sbuf("y_f32", Y_DEPTH, [P, 2, CHUNK], F32)
+        y_bf = sbuf("y_bf", Y_DEPTH, [P, 2, CHUNK], BF16)
+        y_side = sbuf("y_side", 2, [P, 4 * P * PACK], BF16)
+        last_bf = sbuf("last_bf", 2, [P, CHUNK], BF16)
+        last_side = sbuf("last_side", 2, [P, 2 * P * PACK], BF16)
         y_codes = sbuf("y_codes", CHUNKS, [P, T], U32)
         y_plane = sbuf("y_plane", CHUNKS, [P, T], U8)
         ident = keep.tile([P, P], F32, align_bytes=64)
-        sq_banks = tiles(psum, "sq_bank", 4, [P, CHUNK], F32)
-        lin_banks = tiles(psum, "lin_bank", 2, [P, CHUNK], F32)
-        turn_banks = tiles(psum, "turn_bank", 2, [P, CHUNK], F32)
+        im_banks = banks("im_bank", 2)
+        re_banks = banks("re_bank", 2)
+        lin_banks = banks("lin_bank", 2)
+        turn_banks = banks("turn_bank", 2)
 
-        x_src = x_words.rearrange("g p m t -> p g (m t)")
-        c_src = c_words.rearrange("g p n t -> p g (n t)")
-        w_src = w_words.rearrange("g p b -> p g b")
+        def load_words(codes, words, first_byte):
+            width = codes[:].bitcast(U8).shape[2]
+            nc.sync.dma_start(out=codes[:].bitcast(I32), in_=words[:, :, first_byte : first_byte + width].bitcast(I32))
 
-        def load_x(i):
-            a, b = X_LOADS[i]
-            nc.sync.dma_start(out=x_codes[i][:].bitcast(I32), in_=x_src[:, :, PACK * a : PACK * b].bitcast(I32))
+        def load_x(half):
+            load_words(x_codes[half], x_words.rearrange("g p m t -> p g (m t)"), half * X_HALF * PACK)
 
-        def load_c(c):
-            cols = slice(PACK * CHUNK * c, PACK * CHUNK * (c + 1))
-            nc.sync.dma_start(out=c_codes[c][:].bitcast(I32), in_=c_src[:, :, cols].bitcast(I32))
+        def load_c(chunk):
+            load_words(c_codes[chunk], c_words.rearrange("g p n t -> p g (n t)"), chunk * CHUNK * PACK)
 
-        def load_w(c):
-            cols = slice(2 * CHUNK * c, 2 * CHUNK * (c + 1))
-            nc.sync.dma_start(out=w_codes[c][:].bitcast(I32), in_=w_src[:, :, cols].bitcast(I32))
+        def load_w(chunk):
+            load_words(w_codes[chunk], w_words.rearrange("g p b -> p g b"), chunk * CHUNK * 2)
 
-        def load_s(c):
-            for g in range(PASSES):
-                rows = sin_mat[g * P * PACK : (g + 1) * P * PACK, c * CHUNK : (c + 1) * CHUNK]
-                nc.sync.dma_start(out=s_rows[PASSES * c + g][:], in_=rows.rearrange("(p t) n -> p t n", t=PACK))
+        def load_s(j):
+            chunk, g = divmod(j, PASSES)
+            rows = sin_mat[g * P * PACK : (g + 1) * P * PACK, chunk * CHUNK : (chunk + 1) * CHUNK]
+            nc.sync.dma_start(out=s_rows[j][:], in_=rows.rearrange("(p t) n -> p t n", t=PACK))
 
         def load_plane_side_by_side(plane, scales):
-            for q in range(QUADS):
+            for q in QUADRANT_ORDER:
                 nc.sync.dma_start(
-                    out=plane[32 * q : 32 * q + 4, :].bitcast(I32).rearrange("r (g n) -> r g n", g=PASSES),
-                    in_=scales[:, 4 * q : 4 * q + 4, :].bitcast(I32).rearrange("g r n -> r g n"),
+                    out=plane[QUADRANT * q : QUADRANT * q + LIVE, :].bitcast(I32).rearrange("r (g n) -> r g n", g=PASSES),
+                    in_=scales[:, LIVE * q : LIVE * (q + 1), :].bitcast(I32).rearrange("g r n -> r g n"),
                 )
 
-        nc.vector.memset(xc_plane[:].bitcast(U32), 0)
-        nc.vector.memset(w_plane[:].bitcast(U32), 0)
-        nc.vector.memset(ident[:], 0.0)
-        make_identity(nc, ident[:], nomemset=True)
+        def load_c_plane(quadrants):
+            for q in quadrants:
+                row = QUADRANT * q + LIVE
+                nc.sync.dma_start(
+                    out=c_plane[row : row + PASSES * LIVE, :].bitcast(I32),
+                    in_=c_scales[:, LIVE * q : LIVE * (q + 1), :].bitcast(I32),
+                )
 
-        load_plane_side_by_side(xc_plane, x_scales)
-        load_x(0)
+        for plane in (c_plane, w_plane_first, w_plane_rest):
+            nc.vector.memset(plane[:].bitcast(U32), 0)
+        nc.gpsimd.memset(x_plane[:].bitcast(U32), 0)
+        make_identity(nc, ident[:])
+
         load_c(0)
-        for q in range(QUADS):
-            nc.sync.dma_start(
-                out=xc_plane[32 * q + 4 : 32 * q + 12, :N].bitcast(I32),
-                in_=c_scales[:, 4 * q : 4 * q + 4, :].bitcast(I32),
-            )
+        load_plane_side_by_side(x_plane, x_scales)
+        load_c_plane(QUADRANT_ORDER[:2])
+        load_x(0)
+        load_c_plane(QUADRANT_ORDER[2:])
         load_s(0)
-        load_plane_side_by_side(w_plane, w_scales)
         load_w(0)
-        load_x(1)
         load_s(1)
-        load_x(2)
+        load_plane_side_by_side(w_plane_first, w_scales[:, :, :CHUNK])
+        load_x(1)
+        load_s(2)
+        load_plane_side_by_side(w_plane_rest, w_scales[:, :, CHUNK:])
+        load_s(3)
         load_c(1)
         load_w(1)
-        load_s(2)
+        load_s(4)
+        load_s(5)
         load_c(2)
         load_w(2)
 
-        def product(bank, unit, moving):
-            row = unit % TILES
-            i = max(j for j, (a, b) in enumerate(X_LOADS) if a <= row * P)
-            m0 = row * P - X_LOADS[i][0]
+        def c_operand(chunk, g):
+            return c_codes[chunk][:, g, :].bitcast(FP8X4), c_plane[LIVE * (g + 1) :, chunk * CHUNK : (chunk + 1) * CHUNK]
+
+        def s_operand(chunk, g):
+            return s_codes[PASSES * chunk + g][:].bitcast(FP8X4), s_plane[PASSES * chunk + g][:]
+
+        def w_operand(chunk, g):
+            if chunk == 0:
+                plane = w_plane_first[:, g * CHUNK : (g + 1) * CHUNK]
+            else:
+                n0 = g * (N - CHUNK) + (chunk - 1) * CHUNK
+                plane = w_plane_rest[:, n0 : n0 + CHUNK]
+            return w_codes[chunk][:, g, :].bitcast(FP4X4), plane
+
+        def product(bank, unit, operand):
+            chunk, row_tile = divmod(unit, ROW_TILES)
+            half, m0 = divmod(row_tile * P, X_HALF)
             for g in range(PASSES):
-                codes, plane = moving(unit // TILES, g)
+                words, plane = operand(chunk, g)
                 nc.tensor.matmul_mx(
                     out=bank[:],
-                    lhsT=x_codes[i][:, g, m0 : m0 + P].bitcast(FP8X4),
-                    lhsT_scale=xc_plane[:, g * T + row * P : g * T + (row + 1) * P],
-                    rhs=codes,
+                    lhsT=x_codes[half][:, g, m0 : m0 + P].bitcast(FP8X4),
+                    lhsT_scale=x_plane[:, g * T + row_tile * P : g * T + (row_tile + 1) * P],
+                    rhs=words,
                     rhs_scale=plane,
                     start=(g == 0),
                     stop=(g == PASSES - 1),
                 )
 
-        def c_operand(c, g):
-            return c_codes[c][:, g, :].bitcast(FP8X4), xc_plane[4 + 4 * g :, c * CHUNK : (c + 1) * CHUNK]
+        def part_of(unit):
+            return part[unit // 2 % PART_DEPTH][:, unit % 2, :]
 
-        def s_operand(c, g):
-            return s_codes[PASSES * c + g][:].bitcast(FP8X4), s_plane[PASSES * c + g][:]
+        def im_sq_of(unit):
+            return im_sq[unit // 2 % IM_DEPTH][:, unit % 2, :]
 
-        def w_operand(c, g):
-            return w_codes[c][:, g, :].bitcast(FP4X4), w_plane[:, g * N + c * CHUNK : g * N + (c + 1) * CHUNK]
+        def y_of(unit):
+            return y_f32[unit // 2 % Y_DEPTH][:, unit % 2, :]
 
-        def re_bank(u):
-            return sq_banks[(2 * u) % 4]
+        def add(out, in0, in1):
+            nc.vector.tensor_tensor(out=out, in0=in0, in1=in1, op=ADD)
 
-        def im_bank(u):
-            return sq_banks[(2 * u + 1) % 4]
+        def re_squared(unit, bank):
+            product(bank, unit, c_operand)
+            nc.scalar.activation(out=part_of(unit), in_=bank[:], func=SQUARE)
 
-        def square(dst, bank):
-            nc.scalar.activation(out=dst[:], in_=bank[:], func=SQUARE)
+        def im_squared(unit, bank):
+            product(bank, unit, s_operand)
+            nc.scalar.activation(out=im_sq_of(unit), in_=bank[:], func=SQUARE)
 
-        def interleave(copy, j, a, b):
-            copy(
-                out=s_side[j][:, PACK * a : PACK * b].rearrange("p (c i t) -> p c t i", i=4, t=PACK),
-                in_=s_rows[j][:, :, a:b].rearrange("p t (c i) -> p c t i", i=4),
+        def add_lin(unit, bank):
+            add(part_of(unit), bank[:], part_of(unit))
+
+        def interleave_on_vector(j, cols):
+            nc.vector.tensor_copy(
+                out=s_side[j][:, : PACK * cols].rearrange("p (c i t) -> p c t i", i=4, t=PACK),
+                in_=s_rows[j][:, :, :cols].rearrange("p t (c i) -> p c t i", i=4),
+            )
+
+        def interleave_on_scalar(j, cols):
+            nc.scalar.copy(
+                out=s_side[j][:, PACK * cols :].rearrange("p (n t) -> p n t", t=PACK),
+                in_=s_rows[j][:, :, cols:].rearrange("p t n -> p n t"),
             )
 
         def quantise_s(j):
             nc.vector.quantize_mx(out=s_codes[j][:].bitcast(FP8X4), scales=s_plane[j][:], in_=s_side[j][:])
 
-        def add(out, in0, in1):
-            nc.vector.tensor_tensor(out=out, in0=in0, in1=in1, op=ADD)
-
-        def store_y(u):
-            c, row = divmod(u, TILES)
-            nc.sync.dma_start(out=out_0[row * P : (row + 1) * P, c * CHUNK : (c + 1) * CHUNK], in_=y_f32[u % 8][:])
-
-        def pair_sorted(ap):
-            return ap.rearrange("m (p u e) -> m u p e", u=2, e=2)
-
-        def round_y(u):
-            nc.vector.tensor_copy(
-                out=y_bf[u % 8][:].rearrange("m (u p e) -> m u p e", u=2, e=2), in_=pair_sorted(y_f32[u % 8][:])
+        def store_y(first_unit, count):
+            chunk, row_tile = divmod(first_unit, ROW_TILES)
+            rows = out_0[row_tile * P : (row_tile + count) * P, chunk * CHUNK : (chunk + 1) * CHUNK]
+            i0 = first_unit % 2
+            nc.sync.dma_start(
+                out=rows.rearrange("(i m) n -> m i n", m=P),
+                in_=y_f32[first_unit // 2 % Y_DEPTH][:, i0 : i0 + count, :],
             )
 
-        def turn(u, bank, place):
-            words = y_bf[u % 8][:].bitcast(F32)
-            for half in range(2):
-                cols = slice((2 * place + half) * P, (2 * place + half + 1) * P)
-                nc.tensor.transpose(bank[:, cols], words[:, half * P : (half + 1) * P], ident[:])
+        def complete_pair(pair):
+            for i in range(2):
+                im_squared(2 * pair + i, im_banks[i])
+            add(y_f32[pair % Y_DEPTH][:], part[pair % PART_DEPTH][:], im_sq[pair % IM_DEPTH][:])
+            store_y(2 * pair, 2)
+
+        def round_pair(pair):
+            nc.vector.tensor_copy(
+                out=y_bf[pair % Y_DEPTH][:].rearrange("m i (h p e) -> m i h p e", h=2, e=2),
+                in_=y_f32[pair % Y_DEPTH][:].rearrange("m i (p h e) -> m i h p e", h=2, e=2),
+            )
+
+        def by_halves(unit_f32):
+            return unit_f32.rearrange("m (p h e) -> m h p e", h=2, e=2)
+
+        def last_rounded(i):
+            return last_bf[i][:].rearrange("m (h p e) -> m h p e", h=2, e=2)
+
+        def turn(rounded_unit, bank, place):
+            two_value_words = rounded_unit.bitcast(F32)
+            for h in range(2):
+                cols = slice((2 * place + h) * P, (2 * place + h + 1) * P)
+                nc.tensor.transpose(bank[:, cols], two_value_words[:, h * P : (h + 1) * P], ident[:])
+
+        def turn_pair(pair, bank):
+            for i in range(2):
+                turn(y_bf[pair % Y_DEPTH][:, i, :], bank, i)
 
         def empty_turned(bank, count, side, place):
             nc.scalar.copy(
                 out=side[:, place * P * PACK : (place + count) * P * PACK]
                 .bitcast(F32)
-                .rearrange("p (i m u) -> p i m u", u=2, m=P),
-                in_=bank[:, : count * 2 * P].rearrange("p (i u m) -> p i m u", u=2, m=P),
+                .rearrange("p (i m h) -> p i m h", h=2, m=P),
+                in_=bank[:, : count * 2 * P].rearrange("p (i h m) -> p i m h", h=2, m=P),
             )
 
-        def quantise_y(first, count, side):
-            c, row = divmod(first, TILES)
-            toks = slice(row * P, (row + count) * P)
-            nc.vector.quantize_mx(
-                out=y_codes[c][:, toks].bitcast(FP8X4), scales=y_plane[c][:, toks], in_=side[:, : count * P * PACK]
-            )
+        def turn_two_pairs(pair):
+            for i in range(2):
+                turn_pair(pair + i, turn_banks[i])
+            for i in range(2):
+                empty_turned(turn_banks[i], 2, y_side[pair // 2 % 2], 2 * i)
 
-        def store_codes(first, count):
-            c, row = divmod(first, TILES)
-            dst = out_1[c].rearrange("p m t -> p (m t)")[:, PACK * row * P : PACK * (row + count) * P]
-            nc.sync.dma_start(out=dst.bitcast(I32), in_=y_codes[c][:, row * P : (row + count) * P].bitcast(I32))
+        def quantise_y(first_unit, count, side, plane_queues):
+            chunk, row_tile = divmod(first_unit, ROW_TILES)
+            fields = slice(row_tile * P, (row_tile + count) * P)
+            nc.vector.quantize_mx(out=y_codes[chunk][:, fields].bitcast(FP8X4), scales=y_plane[chunk][:, fields], in_=side[:])
+            code_bytes = out_1[chunk].rearrange("p m t -> p (m t)")[:, PACK * fields.start : PACK * fields.stop]
+            nc.sync.dma_start(out=code_bytes.bitcast(I32), in_=y_codes[chunk][:, fields].bitcast(I32))
+            if row_tile + count == ROW_TILES:
+                for q in range(P // QUADRANT):
+                    plane_queues[q % len(plane_queues)].dma_start(
+                        out=out_2[chunk, LIVE * q : LIVE * (q + 1), :].bitcast(I32),
+                        in_=y_plane[chunk][QUADRANT * q : QUADRANT * q + LIVE, :].bitcast(I32),
+                    )
 
-        def store_plane(c, engines):
-            for q in range(QUADS):
-                engines[q % len(engines)].dma_start(
-                    out=out_2[c, 4 * q : 4 * q + 4, :].bitcast(I32),
-                    in_=y_plane[c][32 * q : 32 * q + 4, :].bitcast(I32),
-                )
+        start_re_banks = im_banks + re_banks
+        start_lin_banks = lin_banks + turn_banks
+        re_squared(0, start_re_banks[0])
+        interleave_on_vector(0, VECTOR_COLS_FIRST)
+        interleave_on_scalar(0, VECTOR_COLS_FIRST)
+        re_squared(1, start_re_banks[1])
+        quantise_s(0)
+        interleave_on_vector(1, VECTOR_COLS_FIRST)
+        interleave_on_scalar(1, VECTOR_COLS_FIRST)
+        re_squared(2, start_re_banks[2])
+        re_squared(3, start_re_banks[3])
+        quantise_s(1)
+        for unit in range(4):
+            product(start_lin_banks[unit], unit, w_operand)
+        for unit in range(4):
+            add_lin(unit, start_lin_banks[unit])
 
-        product(re_bank(0), 0, c_operand)
-        square(re_sq[0], re_bank(0))
-        product(re_bank(1), 1, c_operand)
-        for g in range(PASSES):
-            interleave(nc.vector.tensor_copy, g, 0, HEAD_VECTOR_COLS)
-            interleave(nc.scalar.copy, g, HEAD_VECTOR_COLS, CHUNK)
-        square(re_sq[1], re_bank(1))
-        for g in range(PASSES):
-            quantise_s(g)
-        for u in range(2):
-            product(lin_banks[u], u, w_operand)
-            add(re_sq[u][:], lin_banks[u][:], re_sq[u][:])
-        for u in range(2):
-            product(im_bank(u), u, s_operand)
-            square(im_sq[u], im_bank(u))
-            add(y_f32[u][:], re_sq[u][:], im_sq[u][:])
-            store_y(u)
-        round_y(0)
+        last = PAIRS - 1
+        s_steps = [k for k in range(PAIRS) if k == 0 or k % 2 == 1][: PASSES * (CHUNKS - 1)]
+        ahead = 2
+        for k in range(last - 1):
+            complete_pair(k)
+            if k % 2 == 1 and k >= 3:
+                quantise_y(2 * (k - 3), 4, y_side[(k - 3) // 2 % 2], [nc.sync])
+            if k - 1 in s_steps:
+                quantise_s(PASSES + s_steps.index(k - 1))
+            round_pair(k)
+            if k != PAUSE:
+                for i in range(2):
+                    re_squared(2 * ahead + i, re_banks[i])
+            if k % 2 == 0 and k >= 2:
+                turn_two_pairs(k - 2)
+            if k != PAUSE:
+                for i in range(2):
+                    product(lin_banks[i], 2 * ahead + i, w_operand)
+                for i in range(2):
+                    add_lin(2 * ahead + i, lin_banks[i])
+                ahead = ahead + 1
+            if k in s_steps:
+                interleave_on_scalar(PASSES + s_steps.index(k), VECTOR_COLS)
+                interleave_on_vector(PASSES + s_steps.index(k), VECTOR_COLS)
+        assert ahead == last
 
-        run_units = [first + RUN - 1 + RUN_LAG for first in range(0, UNITS - RUN, RUN)]
-        scalar_jobs = {}
-        vector_jobs = {}
-        share = (CHUNK - VECTOR_COLS) // 2
-        for c in range(1, CHUNKS):
-            free = [u for u in range(max(2, (c - 1) * TILES), c * TILES) if u not in run_units]
-            for g in range(PASSES):
-                j = PASSES * c + g
-                scalar_jobs[free[2 * g]] = (j, VECTOR_COLS, VECTOR_COLS + share)
-                scalar_jobs[free[2 * g + 1]] = (j, VECTOR_COLS + share, CHUNK)
-                vector_jobs.setdefault(free[2 * g], []).append(("interleave", j))
-                vector_jobs.setdefault(free[2 * g + 1], []).append(("quantise", j))
-
-        last = UNITS - 1
-        for u in range(2, UNITS):
-            first = u - RUN_LAG - RUN + 1
-            side = y_side[(first // RUN) % 2]
-            if u in run_units:
-                for i in range(RUN):
-                    turn(first + i, turn_banks[i // 2], i % 2)
-                empty_turned(turn_banks[0], 2, side, 0)
-            product(re_bank(u), u, c_operand)
-            square(re_sq[u % 3], re_bank(u))
-            if u in run_units:
-                empty_turned(turn_banks[1], 2, side, 2)
-            product(im_bank(u), u, s_operand)
-            square(im_sq[u % 3], im_bank(u))
-            if u in scalar_jobs:
-                interleave(nc.scalar.copy, *scalar_jobs[u])
-            product(lin_banks[u % 2], u, w_operand)
-            add(re_sq[u % 3][:], re_sq[u % 3][:], im_sq[u % 3][:])
-            round_y(u - 1)
-            if u == last:
-                break
-            add(y_f32[u % 8][:], lin_banks[u % 2][:], re_sq[u % 3][:])
-            store_y(u)
-            if u in run_units:
-                quantise_y(first, RUN, side)
-                store_codes(first, RUN)
-                if (first + RUN) % TILES == 0:
-                    store_plane(first // TILES, [nc.sync])
-            for kind, j in vector_jobs.get(u, []):
-                if kind == "interleave":
-                    interleave(nc.vector.tensor_copy, j, 0, VECTOR_COLS)
-                else:
-                    quantise_s(j)
-
-        side = y_side[((UNITS - RUN) // RUN) % 2]
-        for i in range(2):
-            turn(UNITS - RUN + i, turn_banks[0], i)
-        empty_turned(turn_banks[0], 2, side, 0)
-        add(
-            y_bf[last % 8][:].rearrange("m (u p e) -> m u p e", u=2, e=2),
-            pair_sorted(lin_banks[last % 2][:]),
-            pair_sorted(re_sq[last % 3][:]),
-        )
-        add(y_f32[last % 8][:], lin_banks[last % 2][:], re_sq[last % 3][:])
-        store_y(last)
-        turn(last - 1, turn_banks[1], 0)
-        empty_turned(turn_banks[1], 1, y_side[2], 0)
-        turn(last, sq_banks[0], 0)
-        empty_turned(sq_banks[0], 1, y_side[2], 1)
-        quantise_y(UNITS - RUN, 2, side)
-        store_codes(UNITS - RUN, 2)
-        quantise_y(last - 1, 2, y_side[2])
-        store_codes(last - 1, 2)
-        store_plane(CHUNKS - 1, [nc.scalar, nc.sync])
+        complete_pair(last - 1)
+        turn_two_pairs(last - 3)
+        quantise_y(2 * (last - 3), 4, y_side[(last - 3) // 2 % 2], [nc.sync])
+        round_pair(last - 1)
+        first_of_last, second_of_last = 2 * last, 2 * last + 1
+        for i, unit in enumerate((first_of_last, second_of_last)):
+            re_squared(unit, re_banks[i])
+            product(lin_banks[i], unit, w_operand)
+            im_squared(unit, im_banks[i])
+        for i, unit in enumerate((first_of_last, second_of_last)):
+            add_lin(unit, lin_banks[i])
+        add(y_of(first_of_last), part_of(first_of_last), im_sq_of(first_of_last))
+        store_y(first_of_last, 1)
+        add(last_rounded(1), by_halves(part_of(second_of_last)), by_halves(im_sq_of(second_of_last)))
+        add(y_of(second_of_last), part_of(second_of_last), im_sq_of(second_of_last))
+        store_y(second_of_last, 1)
+        turn_pair(last - 1, turn_banks[0])
+        empty_turned(turn_banks[0], 2, last_side[0], 0)
+        nc.scalar.copy(out=last_rounded(0), in_=by_halves(y_of(first_of_last)))
+        for i in (1, 0):
+            turn(last_bf[i][:], lin_banks[i], 0)
+            empty_turned(lin_banks[i], 1, last_side[1], i)
+        quantise_y(2 * (last - 1), 2, last_side[0], [nc.sync])
+        quantise_y(2 * last, 2, last_side[1], [nc.scalar, nc.sync])

from contextlib import ExitStack

import concourse.mybir as mybir
from concourse.masks import make_identity

T, K, N = 1024, 1024, 1536
FLOPS = 3 * 2 * T * K * N

F32 = mybir.dt.float32
BF16 = mybir.dt.bfloat16
I32 = mybir.dt.int32
U32 = mybir.dt.uint32
U8 = mybir.dt.uint8
FP8X4 = mybir.dt.float8_e4m3fn_x4
FP4X4 = mybir.dt.float4_e2m1fn_x4
ADD = mybir.AluOpType.add
SQUARE = mybir.ActivationFunctionType.Square

P = 128
PACK = 4
PASSES = K // (P * PACK)
CHUNK = 512
CHUNKS = N // CHUNK
ROW_TILES = T // P
PAIRS = CHUNKS * ROW_TILES // 2
X_HALF = T // 2
QUADRANT = 32
LIVE = 4
QUADRANT_ORDER = (0, 2, 1, 3)

VECTOR_COLS_FIRST = 320
VECTOR_COLS = 192
PAUSE = 8

PART_DEPTH = 3
IM_DEPTH = 2
Y_DEPTH = 4


def tile_fresnel_intensity_plus_linear_k3_kernel(
    tc, x_words, x_scales, c_words, c_scales, w_words, w_scales, sin_mat, out_0, out_1, out_2
):
    nc = tc.nc
    with ExitStack() as ctx:
        keep = ctx.enter_context(tc.tile_pool(name="keep", bufs=1))
        psum = ctx.enter_context(tc.psum_pool(name="psum", bufs=1))
        ctx.enter_context(tc.manual_schedule())

        def sbuf(name, count, shape, dtype):
            return [keep.tile(shape, dtype, name="%s%d" % (name, i), align_bytes=64) for i in range(count)]

        def banks(name, count):
            return [psum.tile([P, CHUNK], F32, name="%s%d" % (name, i)) for i in range(count)]

        x_codes = sbuf("x_codes", 2, [P, PASSES, X_HALF], U32)
        c_codes = sbuf("c_codes", CHUNKS, [P, PASSES, CHUNK], U32)
        w_codes = sbuf("w_codes", CHUNKS, [P, PASSES, 2 * CHUNK], U8)
        x_plane = keep.tile([P, PASSES * T], U8, align_bytes=64)
        c_plane = keep.tile([P, N], U8, align_bytes=64)
        w_plane_first = keep.tile([P, PASSES * CHUNK], U8, align_bytes=64)
        w_plane_rest = keep.tile([P, PASSES * (N - CHUNK)], U8, align_bytes=64)
        s_rows = sbuf("s_rows", CHUNKS * PASSES, [P, PACK, CHUNK], BF16)
        s_side = sbuf("s_side", CHUNKS * PASSES, [P, CHUNK * PACK], BF16)
        s_codes = sbuf("s_codes", CHUNKS * PASSES, [P, CHUNK], U32)
        s_plane = sbuf("s_plane", CHUNKS * PASSES, [P, CHUNK], U8)
        part = sbuf("part", PART_DEPTH, [P, 2, CHUNK], F32)
        im_sq = sbuf("im_sq", IM_DEPTH, [P, 2, CHUNK], F32)
        y_f32 = sbuf("y_f32", Y_DEPTH, [P, 2, CHUNK], F32)
        y_bf = sbuf("y_bf", Y_DEPTH, [P, 2, CHUNK], BF16)
        y_side = sbuf("y_side", 2, [P, 4 * P * PACK], BF16)
        last_bf = sbuf("last_bf", 2, [P, CHUNK], BF16)
        last_side = sbuf("last_side", 2, [P, 2 * P * PACK], BF16)
        y_codes = sbuf("y_codes", CHUNKS, [P, T], U32)
        y_plane = sbuf("y_plane", CHUNKS, [P, T], U8)
        ident = keep.tile([P, P], F32, align_bytes=64)
        im_banks = banks("im_bank", 2)
        re_banks = banks("re_bank", 2)
        lin_banks = banks("lin_bank", 2)
        turn_banks = banks("turn_bank", 2)

        def load_words(codes, words, first_byte):
            width = codes[:].bitcast(U8).shape[2]
            nc.sync.dma_start(out=codes[:].bitcast(I32), in_=words[:, :, first_byte : first_byte + width].bitcast(I32))

        def load_x(half):
            load_words(x_codes[half], x_words.rearrange("g p m t -> p g (m t)"), half * X_HALF * PACK)

        def load_c(chunk):
            load_words(c_codes[chunk], c_words.rearrange("g p n t -> p g (n t)"), chunk * CHUNK * PACK)

        def load_w(chunk):
            load_words(w_codes[chunk], w_words.rearrange("g p b -> p g b"), chunk * CHUNK * 2)

        def load_s(j):
            chunk, g = divmod(j, PASSES)
            rows = sin_mat[g * P * PACK : (g + 1) * P * PACK, chunk * CHUNK : (chunk + 1) * CHUNK]
            nc.sync.dma_start(out=s_rows[j][:], in_=rows.rearrange("(p t) n -> p t n", t=PACK))

        def load_plane_side_by_side(plane, scales):
            for q in QUADRANT_ORDER:
                nc.sync.dma_start(
                    out=plane[QUADRANT * q : QUADRANT * q + LIVE, :].bitcast(I32).rearrange("r (g n) -> r g n", g=PASSES),
                    in_=scales[:, LIVE * q : LIVE * (q + 1), :].bitcast(I32).rearrange("g r n -> r g n"),
                )

        def load_c_plane(quadrants):
            for q in quadrants:
                row = QUADRANT * q + LIVE
                nc.sync.dma_start(
                    out=c_plane[row : row + PASSES * LIVE, :].bitcast(I32),
                    in_=c_scales[:, LIVE * q : LIVE * (q + 1), :].bitcast(I32),
                )

        for plane in (c_plane, w_plane_first, w_plane_rest):
            nc.vector.memset(plane[:].bitcast(U32), 0)
        nc.gpsimd.memset(x_plane[:].bitcast(U32), 0)
        make_identity(nc, ident[:])

        load_c(0)
        load_plane_side_by_side(x_plane, x_scales)
        load_c_plane(QUADRANT_ORDER[:2])
        load_x(0)
        load_c_plane(QUADRANT_ORDER[2:])
        load_s(0)
        load_w(0)
        load_s(1)
        load_plane_side_by_side(w_plane_first, w_scales[:, :, :CHUNK])
        load_x(1)
        load_s(2)
        load_plane_side_by_side(w_plane_rest, w_scales[:, :, CHUNK:])
        load_s(3)
        load_c(1)
        load_w(1)
        load_s(4)
        load_s(5)
        load_c(2)
        load_w(2)

        def c_operand(chunk, g):
            return c_codes[chunk][:, g, :].bitcast(FP8X4), c_plane[LIVE * (g + 1) :, chunk * CHUNK : (chunk + 1) * CHUNK]

        def s_operand(chunk, g):
            return s_codes[PASSES * chunk + g][:].bitcast(FP8X4), s_plane[PASSES * chunk + g][:]

        def w_operand(chunk, g):
            if chunk == 0:
                plane = w_plane_first[:, g * CHUNK : (g + 1) * CHUNK]
            else:
                n0 = g * (N - CHUNK) + (chunk - 1) * CHUNK
                plane = w_plane_rest[:, n0 : n0 + CHUNK]
            return w_codes[chunk][:, g, :].bitcast(FP4X4), plane

        def product(bank, unit, operand):
            chunk, row_tile = divmod(unit, ROW_TILES)
            half, m0 = divmod(row_tile * P, X_HALF)
            for g in range(PASSES):
                words, plane = operand(chunk, g)
                nc.tensor.matmul_mx(
                    out=bank[:],
                    lhsT=x_codes[half][:, g, m0 : m0 + P].bitcast(FP8X4),
                    lhsT_scale=x_plane[:, g * T + row_tile * P : g * T + (row_tile + 1) * P],
                    rhs=words,
                    rhs_scale=plane,
                    start=(g == 0),
                    stop=(g == PASSES - 1),
                )

        def part_of(unit):
            return part[unit // 2 % PART_DEPTH][:, unit % 2, :]

        def im_sq_of(unit):
            return im_sq[unit // 2 % IM_DEPTH][:, unit % 2, :]

        def y_of(unit):
            return y_f32[unit // 2 % Y_DEPTH][:, unit % 2, :]

        def add(out, in0, in1):
            nc.vector.tensor_tensor(out=out, in0=in0, in1=in1, op=ADD)

        def re_squared(unit, bank):
            product(bank, unit, c_operand)
            nc.scalar.activation(out=part_of(unit), in_=bank[:], func=SQUARE)

        def im_squared(unit, bank):
            product(bank, unit, s_operand)
            nc.scalar.activation(out=im_sq_of(unit), in_=bank[:], func=SQUARE)

        def add_lin(unit, bank):
            add(part_of(unit), bank[:], part_of(unit))

        def interleave_on_vector(j, cols):
            nc.vector.tensor_copy(
                out=s_side[j][:, : PACK * cols].rearrange("p (c i t) -> p c t i", i=4, t=PACK),
                in_=s_rows[j][:, :, :cols].rearrange("p t (c i) -> p c t i", i=4),
            )

        def interleave_on_scalar(j, cols):
            nc.scalar.copy(
                out=s_side[j][:, PACK * cols :].rearrange("p (n t) -> p n t", t=PACK),
                in_=s_rows[j][:, :, cols:].rearrange("p t n -> p n t"),
            )

        def quantise_s(j):
            nc.vector.quantize_mx(out=s_codes[j][:].bitcast(FP8X4), scales=s_plane[j][:], in_=s_side[j][:])

        def store_y(first_unit, count):
            chunk, row_tile = divmod(first_unit, ROW_TILES)
            rows = out_0[row_tile * P : (row_tile + count) * P, chunk * CHUNK : (chunk + 1) * CHUNK]
            i0 = first_unit % 2
            nc.sync.dma_start(
                out=rows.rearrange("(i m) n -> m i n", m=P),
                in_=y_f32[first_unit // 2 % Y_DEPTH][:, i0 : i0 + count, :],
            )

        def complete_pair(pair):
            for i in range(2):
                im_squared(2 * pair + i, im_banks[i])
            add(y_f32[pair % Y_DEPTH][:], part[pair % PART_DEPTH][:], im_sq[pair % IM_DEPTH][:])
            store_y(2 * pair, 2)

        def round_pair(pair):
            nc.vector.tensor_copy(
                out=y_bf[pair % Y_DEPTH][:].rearrange("m i (h p e) -> m i h p e", h=2, e=2),
                in_=y_f32[pair % Y_DEPTH][:].rearrange("m i (p h e) -> m i h p e", h=2, e=2),
            )

        def by_halves(unit_f32):
            return unit_f32.rearrange("m (p h e) -> m h p e", h=2, e=2)

        def last_rounded(i):
            return last_bf[i][:].rearrange("m (h p e) -> m h p e", h=2, e=2)

        def turn(rounded_unit, bank, place):
            two_value_words = rounded_unit.bitcast(F32)
            for h in range(2):
                cols = slice((2 * place + h) * P, (2 * place + h + 1) * P)
                nc.tensor.transpose(bank[:, cols], two_value_words[:, h * P : (h + 1) * P], ident[:])

        def turn_pair(pair, bank):
            for i in range(2):
                turn(y_bf[pair % Y_DEPTH][:, i, :], bank, i)

        def empty_turned(bank, count, side, place):
            nc.scalar.copy(
                out=side[:, place * P * PACK : (place + count) * P * PACK]
                .bitcast(F32)
                .rearrange("p (i m h) -> p i m h", h=2, m=P),
                in_=bank[:, : count * 2 * P].rearrange("p (i h m) -> p i m h", h=2, m=P),
            )

        def turn_two_pairs(pair):
            for i in range(2):
                turn_pair(pair + i, turn_banks[i])
            for i in range(2):
                empty_turned(turn_banks[i], 2, y_side[pair // 2 % 2], 2 * i)

        def quantise_y(first_unit, count, side, plane_queues):
            chunk, row_tile = divmod(first_unit, ROW_TILES)
            fields = slice(row_tile * P, (row_tile + count) * P)
            nc.vector.quantize_mx(out=y_codes[chunk][:, fields].bitcast(FP8X4), scales=y_plane[chunk][:, fields], in_=side[:])
            code_bytes = out_1[chunk].rearrange("p m t -> p (m t)")[:, PACK * fields.start : PACK * fields.stop]
            nc.sync.dma_start(out=code_bytes.bitcast(I32), in_=y_codes[chunk][:, fields].bitcast(I32))
            if row_tile + count == ROW_TILES:
                for q in range(P // QUADRANT):
                    plane_queues[q % len(plane_queues)].dma_start(
                        out=out_2[chunk, LIVE * q : LIVE * (q + 1), :].bitcast(I32),
                        in_=y_plane[chunk][QUADRANT * q : QUADRANT * q + LIVE, :].bitcast(I32),
                    )

        start_re_banks = im_banks + re_banks
        start_lin_banks = lin_banks + turn_banks
        re_squared(0, start_re_banks[0])
        interleave_on_vector(0, VECTOR_COLS_FIRST)
        interleave_on_scalar(0, VECTOR_COLS_FIRST)
        re_squared(1, start_re_banks[1])
        quantise_s(0)
        interleave_on_vector(1, VECTOR_COLS_FIRST)
        interleave_on_scalar(1, VECTOR_COLS_FIRST)
        re_squared(2, start_re_banks[2])
        re_squared(3, start_re_banks[3])
        quantise_s(1)
        for unit in range(4):
            product(start_lin_banks[unit], unit, w_operand)
        for unit in range(4):
            add_lin(unit, start_lin_banks[unit])

        last = PAIRS - 1
        s_steps = [k for k in range(PAIRS) if k == 0 or k % 2 == 1][: PASSES * (CHUNKS - 1)]
        ahead = 2
        for k in range(last - 1):
            complete_pair(k)
            if k % 2 == 1 and k >= 3:
                quantise_y(2 * (k - 3), 4, y_side[(k - 3) // 2 % 2], [nc.sync])
            if k - 1 in s_steps:
                quantise_s(PASSES + s_steps.index(k - 1))
            round_pair(k)
            if k != PAUSE:
                for i in range(2):
                    re_squared(2 * ahead + i, re_banks[i])
            if k % 2 == 0 and k >= 2:
                turn_two_pairs(k - 2)
            if k != PAUSE:
                for i in range(2):
                    product(lin_banks[i], 2 * ahead + i, w_operand)
                for i in range(2):
                    add_lin(2 * ahead + i, lin_banks[i])
                ahead = ahead + 1
            if k in s_steps:
                interleave_on_scalar(PASSES + s_steps.index(k), VECTOR_COLS)
                interleave_on_vector(PASSES + s_steps.index(k), VECTOR_COLS)
        assert ahead == last

        complete_pair(last - 1)
        turn_two_pairs(last - 3)
        quantise_y(2 * (last - 3), 4, y_side[(last - 3) // 2 % 2], [nc.sync])
        round_pair(last - 1)
        first_of_last, second_of_last = 2 * last, 2 * last + 1
        for i, unit in enumerate((first_of_last, second_of_last)):
            re_squared(unit, re_banks[i])
            product(lin_banks[i], unit, w_operand)
            im_squared(unit, im_banks[i])
        for i, unit in enumerate((first_of_last, second_of_last)):
            add_lin(unit, lin_banks[i])
        add(y_of(first_of_last), part_of(first_of_last), im_sq_of(first_of_last))
        store_y(first_of_last, 1)
        add(last_rounded(1), by_halves(part_of(second_of_last)), by_halves(im_sq_of(second_of_last)))
        add(y_of(second_of_last), part_of(second_of_last), im_sq_of(second_of_last))
        store_y(second_of_last, 1)
        turn_pair(last - 1, turn_banks[0])
        empty_turned(turn_banks[0], 2, last_side[0], 0)
        nc.scalar.copy(out=last_rounded(0), in_=by_halves(y_of(first_of_last)))
        for i in (1, 0):
            turn(last_bf[i][:], lin_banks[i], 0)
            empty_turned(lin_banks[i], 1, last_side[1], i)
        quantise_y(2 * (last - 1), 2, last_side[0], [nc.sync])
        quantise_y(2 * last, 2, last_side[1], [nc.scalar, nc.sync])
